import numpy as np
import ml_dtypes


def mxq(x, axis, fmt="e4m3"):
    dtype, down = {"e4m3": (ml_dtypes.float8_e4m3fn, 7), "e5m2": (ml_dtypes.float8_e5m2, 14)}[fmt]
    v = np.moveaxis(np.asarray(x, np.float32).astype(ml_dtypes.bfloat16).astype(np.float64), axis, -1)
    blocks = v.reshape(v.shape[:-1] + (-1, 32))
    amax = np.abs(blocks).max(-1, keepdims=True)
    byte = np.maximum(np.where(amax > 0, np.frexp(amax)[1] - 1 + 127, 0) - down, 1)
    scale = np.exp2(byte - 127.0)
    codes = (blocks / scale).astype(np.float32).astype(dtype).astype(np.float64)
    return np.moveaxis((codes * scale).reshape(v.shape), -1, axis)


WIDE = False


def mx_kscale(k):
    if not WIDE:
        return np.ones(k)
    levels = np.array([10, -10, 5, -5, 0])
    if k % 512:
        return np.exp2(np.random.permutation(np.resize(levels, k // 32))).repeat(32)
    a = np.empty((k // 512, 16))
    for p in range(k // 512):
        a[p, :8] = np.random.permutation(np.resize(levels, 8))
        for g in range(8):
            far = levels[np.abs(levels - a[p, g]) >= 10]
            a[p, g + 8] = far[np.random.randint(len(far))]
    return np.exp2(a.ravel()).repeat(32)


def f64(x):
    return np.asarray(x).astype(np.float64)


def striped(idx):
    return np.tile(idx.reshape(-1, 16).T, (8, 1)).astype(np.uint16)


def unstriped(offs):
    return offs[:16].T.reshape(-1).astype(np.int64)


def pack_weight(w):
    k, n = w.shape
    w = f64(np.asarray(w, np.float32).astype(ml_dtypes.bfloat16)).reshape(k // 32, 32, n)
    amax = np.abs(w).max(1)
    byte = np.clip(np.where(amax > 0, np.frexp(amax)[1] - 1 + 127 - 7, 1), 1, 254)
    scaled = (w * np.exp2(127.0 - byte)[:, None, :]).reshape(k, n).astype(np.float32)
    words = np.ascontiguousarray(scaled.reshape(k // 512, 128, 4, n).transpose(0, 1, 3, 2)).astype(ml_dtypes.float8_e4m3fn).view(np.uint8)
    return words, np.ascontiguousarray(byte.astype(np.uint8).reshape(k // 512, 16, n))


def unpack_weight(words, scales):
    g, p, n, _ = words.shape
    vals = np.ascontiguousarray(words).view(ml_dtypes.float8_e4m3fn).astype(np.float64) * np.repeat(np.exp2(scales.astype(np.float64) - 127.0), 8, axis=1)[..., None]
    return vals.transpose(0, 1, 3, 2).reshape(g * 512, n)


K, T, S, H, N = 512, 4096, 1024, 512, 256


def setup_inputs():
    n = np.random.standard_normal
    s = mx_kscale(K)[:, None]
    u = mx_kscale(H)
    packed_xT = pack_weight(n((K, T)) * s)
    return {
        "x_words": packed_xT[0],
        "x_scales": packed_xT[1],
        "w1": (n((K, N)) / np.sqrt(2 * K) / s).astype(np.float32),
        "w2": (n((K, H)) / np.sqrt(K) / s * u).astype(np.float32),
        "w3": (n((H, N)) / np.sqrt(2 * H) / u[:, None]).astype(np.float32),
        "offs": striped(np.random.permutation(T)[:S]),
    }


def reference(x_words, x_scales, w1, w2, w3, offs):
    xq = unpack_weight(x_words, x_scales)[:, unstriped(offs)]
    h = mxq(f64(w2), 0, "e4m3").T @ xq
    return mxq(f64(w1), 0, "e4m3").T @ xq + mxq(f64(w3), 0, "e4m3").T @ mxq(h, 0, "e4m3")

@@ -1,0 +1,190 @@
+from contextlib import ExitStack
+
+import concourse.mybir as mybir
+
+K, T, S, H, N = 512, 4096, 1024, 512, 256
+FLOPS = 2 * S * (K * H + K * N + H * N)
+
+F32 = mybir.dt.float32
+BF16 = mybir.dt.bfloat16
+I32 = mybir.dt.int32
+U32 = mybir.dt.uint32
+U16 = mybir.dt.uint16
+U8 = mybir.dt.uint8
+FP8X4 = mybir.dt.float8_e4m3fn_x4
+
+P = 128
+PACK = 4
+H_TOK = 128
+OUT_TOK = 256
+GATHER = 512
+W2_VECTOR = 88
+H_ON_VECTOR = (0, 4, 6,)
+
+
+def copy_on(nc, on_vector, out, in_):
+    if on_vector:
+        nc.vector.tensor_copy(out=out, in_=in_)
+    else:
+        nc.scalar.copy(out=out, in_=in_)
+
+
+def tile_picked_lora_none_p_kernel(tc, x_words, x_scales, w1, w2, w3, offs, out):
+    nc = tc.nc
+    with ExitStack() as ctx:
+        keep = ctx.enter_context(tc.tile_pool(name="keep", bufs=1))
+        psum = ctx.enter_context(tc.psum_pool(name="psum", bufs=1))
+
+        offsets = keep.tile([P, S // 16], U16, name="offsets")
+        all_words = keep.tile([P, T], U32, name="all_words", align_bytes=64)
+        all_scales = keep.tile([P, T], U8, name="all_scales", tag="scales_then_weights", align_bytes=64)
+        w2_raw = keep.tile([P, PACK, H], F32, name="w2_raw", align_bytes=64)
+
+        x_codes = keep.tile([P, S], U32, name="x_codes", align_bytes=64)
+        picked_scales = keep.tile([P, S], U8, name="picked_scales", align_bytes=64)
+        x_scale = keep.tile([P, S], U8, name="x_scale", align_bytes=64)
+
+        nc.sync.dma_start(out=all_scales[P - 16 :, :].bitcast(I32), in_=x_scales[0].bitcast(I32))
+        nc.sync.dma_start(offsets[:], offs)
+        nc.sync.dma_start(
+            out=all_words[:].bitcast(I32),
+            in_=x_words[0].rearrange("p c r -> p (c r)").bitcast(I32),
+        )
+        nc.sync.dma_start(out=w2_raw[:], in_=w2.rearrange("(p j) c -> p j c", j=PACK))
+        nc.vector.memset(all_scales[: P - 16, :].bitcast(I32), 0)
+        nc.vector.memset(x_scale[:].bitcast(I32), 0)
+
+        nc.vector.tensor_copy(picked_scales[:], all_scales[:].indirect(offsets[:]))
+        for q in range(4):
+            nc.sync.dma_start(
+                out=x_scale[32 * q : 32 * q + 4, :].bitcast(I32),
+                in_=picked_scales[P - 16 + 4 * q : P - 12 + 4 * q, :].bitcast(I32),
+            )
+        w31_raw = keep.tile([P, 2 * PACK * N], F32, name="w31_raw", tag="scales_then_weights", align_bytes=64)
+        w3_raw = w31_raw[:, : PACK * N]
+        w1_raw = w31_raw[:, PACK * N :]
+        for raw, w in ((w3_raw, w3), (w1_raw, w1)):
+            nc.sync.dma_start(out=raw, in_=w.rearrange("(p j) c -> p (j c)", j=PACK))
+
+        for g in range(S // GATHER):
+            cols = GATHER // 16
+            nc.vector.tensor_copy(
+                x_codes[:, g * GATHER : (g + 1) * GATHER],
+                all_words[:].indirect(offsets[:, g * cols : (g + 1) * cols]),
+            )
+
+        w2_bf = keep.tile([P, PACK, P, PACK], BF16, name="w2_bf", align_bytes=64)
+        w2_codes = keep.tile([P, H], U32, name="w2_codes", align_bytes=64)
+        w2_scale = keep.tile([P, H], U8, name="w2_scale", align_bytes=64)
+        w2_dst = w2_bf[:].rearrange("p t m j -> p m j t")
+        w2_src = w2_raw[:].rearrange("p j (m t) -> p m j t", t=PACK)
+        nc.scalar.copy(out=w2_dst[:, W2_VECTOR:], in_=w2_src[:, W2_VECTOR:])
+        nc.vector.tensor_copy(out=w2_dst[:, :W2_VECTOR], in_=w2_src[:, :W2_VECTOR])
+        for t in range(PACK):
+            nc.vector.quantize_mx(
+                out=w2_codes[:, t * P : (t + 1) * P].bitcast(FP8X4),
+                scales=w2_scale[:, t * P : (t + 1) * P],
+                in_=w2_bf[:, t].rearrange("p m j -> p (m j)"),
+            )
+
+        def out_weight(raw, name):
+            bf = keep.tile([P, N, PACK], BF16, name=name + "_bf", align_bytes=64)
+            codes = keep.tile([P, N], U32, name=name + "_codes", align_bytes=64)
+            scale = keep.tile([P, N], U8, name=name + "_scale", align_bytes=64)
+            dst = bf[:].rearrange("p (c i) j -> p c j i", i=4)
+            src = raw.rearrange("p (j c i) -> p c j i", j=PACK, i=4)
+            return bf, codes, scale, dst, src
+
+        def quantize_weight(bf, codes, scale):
+            nc.vector.quantize_mx(out=codes[:].bitcast(FP8X4), scales=scale[:], in_=bf[:].rearrange("p c j -> p (c j)"))
+
+        w3_bf, w3_codes, w3_scale, w3_dst, w3_src = out_weight(w3_raw, "w3")
+        w1_bf, w1_codes, w1_scale, w1_dst, w1_src = out_weight(w1_raw, "w1")
+
+        h_bf = keep.tile([P, S, PACK], BF16, name="h_bf", align_bytes=64)
+        h_codes = keep.tile([P, S], U32, name="h_codes", align_bytes=64)
+        h_scale = keep.tile([P, S], U8, name="h_scale", align_bytes=64)
+        result = [keep.tile([P, N // P, OUT_TOK], F32, name="result%d" % c, align_bytes=64) for c in range(S // OUT_TOK)]
+        out_view = out.rearrange("(m p) s -> p m s", p=P)
+
+        def hidden(b):
+            tok = slice(b * H_TOK, (b + 1) * H_TOK)
+            bank = psum.tile([P, PACK, H_TOK], F32, name="h_bank", tag="h_bank", bufs=5)
+            for t in range(PACK):
+                cols = slice(t * P, (t + 1) * P)
+                nc.tensor.matmul_mx(
+                    out=bank[:, t, :],
+                    lhsT=w2_codes[:, cols].bitcast(FP8X4),
+                    lhsT_scale=w2_scale[:, cols],
+                    rhs=x_codes[:, tok].bitcast(FP8X4),
+                    rhs_scale=x_scale[:, tok],
+                    start=True,
+                    stop=True,
+                )
+            copy_on(nc, b in H_ON_VECTOR, h_bf[:, tok, :], bank[:].rearrange("p t s -> p s t"))
+
+        def quantize_hidden(c):
+            tok = slice(c * OUT_TOK, (c + 1) * OUT_TOK)
+            nc.vector.quantize_mx(
+                out=h_codes[:, tok].bitcast(FP8X4),
+                scales=h_scale[:, tok],
+                in_=h_bf[:, tok, :].rearrange("p s t -> p (s t)"),
+            )
+
+        def out_group(acc, m, tok):
+            cols = slice(m * P, (m + 1) * P)
+            nc.tensor.matmul_mx(
+                out=acc,
+                lhsT=w1_codes[:, cols].bitcast(FP8X4),
+                lhsT_scale=w1_scale[:, cols],
+                rhs=x_codes[:, tok].bitcast(FP8X4),
+                rhs_scale=x_scale[:, tok],
+                start=True,
+                stop=False,
+            )
+            nc.tensor.matmul_mx(
+                out=acc,
+                lhsT=w3_codes[:, cols].bitcast(FP8X4),
+                lhsT_scale=w3_scale[:, cols],
+                rhs=h_codes[:, tok].bitcast(FP8X4),
+                rhs_scale=h_scale[:, tok],
+                start=False,
+                stop=True,
+            )
+
+        def output(c, on_vector):
+            tok = slice(c * OUT_TOK, (c + 1) * OUT_TOK)
+            bank = psum.tile([P, N // P, OUT_TOK], F32, name="out_bank", tag="out_bank", bufs=3)
+            for m in range(N // P):
+                out_group(bank[:, m, :], m, tok)
+            copy_on(nc, on_vector, result[c][:], bank[:])
+            nc.sync.dma_start(out=out_view[:, :, tok], in_=result[c][:])
+
+        def last_output(c):
+            tok = slice(c * OUT_TOK, (c + 1) * OUT_TOK)
+            for m in range(N // P):
+                bank = psum.tile([P, OUT_TOK], F32, name="last_bank", tag="h_bank", bufs=5)
+                out_group(bank[:], m, tok)
+                copy_on(nc, m == 1, result[c][:, m, :], bank[:])
+            nc.sync.dma_start(out=out_view[:, :, tok], in_=result[c][:])
+
+        nc.scalar.copy(out=w3_dst, in_=w3_src)
+        hidden(0)
+        hidden(1)
+        nc.vector.tensor_copy(out=w1_dst, in_=w1_src)
+        quantize_weight(w3_bf, w3_codes, w3_scale)
+        quantize_weight(w1_bf, w1_codes, w1_scale)
+        hidden(2)
+        hidden(3)
+        quantize_hidden(0)
+        hidden(4)
+        hidden(5)
+        quantize_hidden(1)
+        output(0, False)
+        hidden(6)
+        hidden(7)
+        quantize_hidden(2)
+        output(1, False)
+        quantize_hidden(3)
+        output(2, True)
+        last_output(3)

@@ -15,176 +15,203 @@ FP8X4 = mybir.dt.float8_e4m3fn_x4
 
 P = 128
 PACK = 4
-H_TOK = 128
-OUT_TOK = 256
+ALIGN = 64
+SCALE_ROWS = K // 32
+QUADRANT = 32
+LIST_ROWS = 16
 GATHER = 512
-W2_VECTOR = 88
-H_ON_VECTOR = (0, 4, 6,)
+BLOCK = 128
+LINE = 4
+
+CHUNKS = (256, 256, 256, 128, 128)
+
+BLOCKS_ON_VECTOR = (2, 5, 7)
+CHUNK_ON_VECTOR = 3
+
+W3_GROUPS_ON_VECTOR = 28
+
+WARM_UP_PASSES = 3
+
+RAW_BYTES = PACK * N * 4
+H_BYTES = [n * PACK * 2 for n in CHUNKS]
+W3_RAW_AT = 0
+W1_RAW_AT = RAW_BYTES
+SCALES_AT = RAW_BYTES // 2
+H2_AT = W1_RAW_AT + ALIGN - H_BYTES[2]
+H1_AT = H2_AT + H_BYTES[2]
+H4_AT = H1_AT + H_BYTES[1]
+H_WORDS_AT = H4_AT + H_BYTES[4]
+W1_BF_AT = H_WORDS_AT + S * 4
+H_AT = (W3_RAW_AT, H1_AT, H2_AT, W1_BF_AT, H4_AT)
 
 
-def copy_on(nc, on_vector, out, in_):
+def copy_out_of_psum(nc, on_vector, out, in_):
     if on_vector:
         nc.vector.tensor_copy(out=out, in_=in_)
     else:
         nc.scalar.copy(out=out, in_=in_)
 
 
+def quantize(nc, words, scales, values):
+    nc.vector.quantize_mx(out=words.bitcast(FP8X4), scales=scales, in_=values)
+
+
+def mx_pass(nc, acc, stationary, stationary_cols, moving, moving_cols, start, stop):
+    nc.tensor.matmul_mx(
+        out=acc,
+        lhsT=stationary[0][:, stationary_cols].bitcast(FP8X4),
+        lhsT_scale=stationary[1][:, stationary_cols],
+        rhs=moving[0][:, moving_cols].bitcast(FP8X4),
+        rhs_scale=moving[1][:, moving_cols],
+        start=start,
+        stop=stop,
+    )
+
+
 def tile_picked_lora_none_p_kernel(tc, x_words, x_scales, w1, w2, w3, offs, out):
     nc = tc.nc
     with ExitStack() as ctx:
         keep = ctx.enter_context(tc.tile_pool(name="keep", bufs=1))
+        shared = ctx.enter_context(tc.tile_pool(name="shared", bufs=1))
         psum = ctx.enter_context(tc.psum_pool(name="psum", bufs=1))
 
-        offsets = keep.tile([P, S // 16], U16, name="offsets")
-        all_words = keep.tile([P, T], U32, name="all_words", align_bytes=64)
-        all_scales = keep.tile([P, T], U8, name="all_scales", tag="scales_then_weights", align_bytes=64)
-        w2_raw = keep.tile([P, PACK, H], F32, name="w2_raw", align_bytes=64)
+        offsets = keep.tile([P, S // LIST_ROWS], U16, name="offsets")
+        all_words = keep.tile([P, T], U32, name="all_words", align_bytes=ALIGN)
+        all_scales = shared.tile([P, T], U8, name="all_scales", align_bytes=ALIGN, offset=SCALES_AT)
+        w2_raw = [keep.tile([P, PACK, H // 2], F32, name="w2_raw%d" % u, align_bytes=ALIGN) for u in range(2)]
+        picked_words = keep.tile([P, S], U32, name="picked_words", align_bytes=ALIGN)
+        picked_rows = keep.tile([P, S], U8, name="picked_rows", align_bytes=ALIGN)
+        picked_scales = keep.tile([P, S], U8, name="picked_scales", align_bytes=ALIGN)
 
-        x_codes = keep.tile([P, S], U32, name="x_codes", align_bytes=64)
-        picked_scales = keep.tile([P, S], U8, name="picked_scales", align_bytes=64)
-        x_scale = keep.tile([P, S], U8, name="x_scale", align_bytes=64)
-
-        nc.sync.dma_start(out=all_scales[P - 16 :, :].bitcast(I32), in_=x_scales[0].bitcast(I32))
+        first_row = P - SCALE_ROWS
+        nc.sync.dma_start(out=all_scales[first_row:, :].bitcast(I32), in_=x_scales[0].bitcast(I32))
         nc.sync.dma_start(offsets[:], offs)
         nc.sync.dma_start(
             out=all_words[:].bitcast(I32),
             in_=x_words[0].rearrange("p c r -> p (c r)").bitcast(I32),
         )
-        nc.sync.dma_start(out=w2_raw[:], in_=w2.rearrange("(p j) c -> p j c", j=PACK))
-        nc.vector.memset(all_scales[: P - 16, :].bitcast(I32), 0)
-        nc.vector.memset(x_scale[:].bitcast(I32), 0)
+        w2_rows = w2.rearrange("(p j) c -> p j c", j=PACK)
+        for u in range(2):
+            nc.sync.dma_start(out=w2_raw[u][:], in_=w2_rows[:, :, u * (H // 2) : (u + 1) * (H // 2)])
+        nc.vector.memset(all_scales[:first_row, :].bitcast(I32), 0)
+        nc.vector.memset(picked_scales[:].bitcast(I32), 0)
 
-        nc.vector.tensor_copy(picked_scales[:], all_scales[:].indirect(offsets[:]))
-        for q in range(4):
+        nc.vector.tensor_copy(picked_rows[:], all_scales[:].indirect(offsets[:]))
+        rows = SCALE_ROWS * QUADRANT // P
+        for q in range(P // QUADRANT):
             nc.sync.dma_start(
-                out=x_scale[32 * q : 32 * q + 4, :].bitcast(I32),
-                in_=picked_scales[P - 16 + 4 * q : P - 12 + 4 * q, :].bitcast(I32),
+                out=picked_scales[QUADRANT * q : QUADRANT * q + rows, :].bitcast(I32),
+                in_=picked_rows[first_row + rows * q : first_row + rows * (q + 1), :].bitcast(I32),
             )
-        w31_raw = keep.tile([P, 2 * PACK * N], F32, name="w31_raw", tag="scales_then_weights", align_bytes=64)
-        w3_raw = w31_raw[:, : PACK * N]
-        w1_raw = w31_raw[:, PACK * N :]
+        w3_raw = shared.tile([P, PACK * N], F32, name="w3_raw", align_bytes=ALIGN, offset=W3_RAW_AT)
+        w1_raw = shared.tile([P, PACK * N], F32, name="w1_raw", align_bytes=ALIGN, offset=W1_RAW_AT)
         for raw, w in ((w3_raw, w3), (w1_raw, w1)):
-            nc.sync.dma_start(out=raw, in_=w.rearrange("(p j) c -> p (j c)", j=PACK))
+            nc.sync.dma_start(out=raw[:], in_=w.rearrange("(p j) c -> p (j c)", j=PACK))
 
+        list_cols = GATHER // LIST_ROWS
         for g in range(S // GATHER):
-            cols = GATHER // 16
             nc.vector.tensor_copy(
-                x_codes[:, g * GATHER : (g + 1) * GATHER],
-                all_words[:].indirect(offsets[:, g * cols : (g + 1) * cols]),
+                picked_words[:, g * GATHER : (g + 1) * GATHER],
+                all_words[:].indirect(offsets[:, g * list_cols : (g + 1) * list_cols]),
             )
+        x_mx = (picked_words, picked_scales)
 
-        w2_bf = keep.tile([P, PACK, P, PACK], BF16, name="w2_bf", align_bytes=64)
-        w2_codes = keep.tile([P, H], U32, name="w2_codes", align_bytes=64)
-        w2_scale = keep.tile([P, H], U8, name="w2_scale", align_bytes=64)
+        blocks = S // BLOCK
+        warm_up = psum.tile([P, GATHER], F32, name="warm_up", tag="bank%d" % (blocks - 1))
+        first_words = (picked_words, picked_rows)
+        for i in range(WARM_UP_PASSES):
+            mx_pass(nc, warm_up[:], first_words, slice(0, P), first_words, slice(0, GATHER), True, True)
+
+        w2_bf = keep.tile([P, PACK, P, PACK], BF16, name="w2_bf", align_bytes=ALIGN)
+        w2_words = keep.tile([P, H], U32, name="w2_words", align_bytes=ALIGN)
+        w2_scales = keep.tile([P, H], U8, name="w2_scales", align_bytes=ALIGN)
         w2_dst = w2_bf[:].rearrange("p t m j -> p m j t")
-        w2_src = w2_raw[:].rearrange("p j (m t) -> p m j t", t=PACK)
-        nc.scalar.copy(out=w2_dst[:, W2_VECTOR:], in_=w2_src[:, W2_VECTOR:])
-        nc.vector.tensor_copy(out=w2_dst[:, :W2_VECTOR], in_=w2_src[:, :W2_VECTOR])
-        for t in range(PACK):
-            nc.vector.quantize_mx(
-                out=w2_codes[:, t * P : (t + 1) * P].bitcast(FP8X4),
-                scales=w2_scale[:, t * P : (t + 1) * P],
-                in_=w2_bf[:, t].rearrange("p m j -> p (m j)"),
-            )
+        w2_src = [raw[:].rearrange("p j (m t) -> p m j t", t=PACK) for raw in w2_raw]
+        nc.scalar.copy(out=w2_dst[:, : P // 2], in_=w2_src[0])
+        nc.scalar.copy(out=w2_dst[:, P // 2 :, :, :2], in_=w2_src[1][:, :, :, :2])
+        nc.vector.tensor_copy(out=w2_dst[:, P // 2 :, :, 2:], in_=w2_src[1][:, :, :, 2:])
+        for t in (0, 2):
+            cols = slice(t * P, (t + 2) * P)
+            quantize(nc, w2_words[:, cols], w2_scales[:, cols], w2_bf[:, t : t + 2].rearrange("p t m j -> p (t m j)"))
+        w2_mx = (w2_words, w2_scales)
 
-        def out_weight(raw, name):
-            bf = keep.tile([P, N, PACK], BF16, name=name + "_bf", align_bytes=64)
-            codes = keep.tile([P, N], U32, name=name + "_codes", align_bytes=64)
-            scale = keep.tile([P, N], U8, name=name + "_scale", align_bytes=64)
-            dst = bf[:].rearrange("p (c i) j -> p c j i", i=4)
-            src = raw.rearrange("p (j c i) -> p c j i", j=PACK, i=4)
-            return bf, codes, scale, dst, src
+        w3_bf = keep.tile([P, N, PACK], BF16, name="w3_bf", align_bytes=ALIGN)
+        w3_words = keep.tile([P, N], U32, name="w3_words", align_bytes=ALIGN)
+        w3_scales = keep.tile([P, N], U8, name="w3_scales", align_bytes=ALIGN)
+        w1_bf = shared.tile([P, N, PACK], BF16, name="w1_bf", align_bytes=ALIGN, offset=W1_BF_AT)
+        w1_words = keep.tile([P, N], U32, name="w1_words", align_bytes=ALIGN)
+        w1_scales = keep.tile([P, N], U8, name="w1_scales", align_bytes=ALIGN)
+        w3_dst, w1_dst = [bf[:].rearrange("p (c i) j -> p c j i", i=LINE) for bf in (w3_bf, w1_bf)]
+        w3_src, w1_src = [raw[:].rearrange("p (j c i) -> p c j i", j=PACK, i=LINE) for raw in (w3_raw, w1_raw)]
+        w3_mx = (w3_words, w3_scales)
+        w1_mx = (w1_words, w1_scales)
 
-        def quantize_weight(bf, codes, scale):
-            nc.vector.quantize_mx(out=codes[:].bitcast(FP8X4), scales=scale[:], in_=bf[:].rearrange("p c j -> p (c j)"))
+        nc.scalar.copy(out=w3_dst[:, W3_GROUPS_ON_VECTOR:], in_=w3_src[:, W3_GROUPS_ON_VECTOR:])
+        nc.vector.tensor_copy(out=w3_dst[:, :W3_GROUPS_ON_VECTOR], in_=w3_src[:, :W3_GROUPS_ON_VECTOR])
+        quantize(nc, w3_words[:], w3_scales[:], w3_bf[:].rearrange("p c j -> p (c j)"))
 
-        w3_bf, w3_codes, w3_scale, w3_dst, w3_src = out_weight(w3_raw, "w3")
-        w1_bf, w1_codes, w1_scale, w1_dst, w1_src = out_weight(w1_raw, "w1")
-
-        h_bf = keep.tile([P, S, PACK], BF16, name="h_bf", align_bytes=64)
-        h_codes = keep.tile([P, S], U32, name="h_codes", align_bytes=64)
-        h_scale = keep.tile([P, S], U8, name="h_scale", align_bytes=64)
-        result = [keep.tile([P, N // P, OUT_TOK], F32, name="result%d" % c, align_bytes=64) for c in range(S // OUT_TOK)]
+        h_bf = [
+            shared.tile([P, n, PACK], BF16, name="h_bf%d" % c, align_bytes=ALIGN, offset=H_AT[c])
+            for c, n in enumerate(CHUNKS)
+        ]
+        h_words = shared.tile([P, S], U32, name="h_words", align_bytes=ALIGN, offset=H_WORDS_AT)
+        h_scales = keep.tile([P, S], U8, name="h_scales", align_bytes=ALIGN)
+        h_mx = (h_words, h_scales)
+        result = [keep.tile([P, N // P, n], F32, name="result%d" % c, align_bytes=ALIGN) for c, n in enumerate(CHUNKS)]
         out_view = out.rearrange("(m p) s -> p m s", p=P)
+        starts = [sum(CHUNKS[:c]) for c in range(len(CHUNKS))]
+
+        def tokens(c):
+            return slice(starts[c], starts[c] + CHUNKS[c])
 
         def hidden(b):
-            tok = slice(b * H_TOK, (b + 1) * H_TOK)
-            bank = psum.tile([P, PACK, H_TOK], F32, name="h_bank", tag="h_bank", bufs=5)
+            first = b * BLOCK
+            bank = psum.tile([P, PACK, BLOCK], F32, name="h_bank", tag="bank%d" % b)
             for t in range(PACK):
-                cols = slice(t * P, (t + 1) * P)
-                nc.tensor.matmul_mx(
-                    out=bank[:, t, :],
-                    lhsT=w2_codes[:, cols].bitcast(FP8X4),
-                    lhsT_scale=w2_scale[:, cols],
-                    rhs=x_codes[:, tok].bitcast(FP8X4),
-                    rhs_scale=x_scale[:, tok],
-                    start=True,
-                    stop=True,
-                )
-            copy_on(nc, b in H_ON_VECTOR, h_bf[:, tok, :], bank[:].rearrange("p t s -> p s t"))
+                mx_pass(nc, bank[:, t, :], w2_mx, slice(t * P, (t + 1) * P), x_mx, slice(first, first + BLOCK), True, True)
+            c = max(i for i, start in enumerate(starts) if start <= first)
+            dst = h_bf[c][:, first - starts[c] : first - starts[c] + BLOCK, :]
+            copy_out_of_psum(nc, b in BLOCKS_ON_VECTOR, dst, bank[:].rearrange("p t s -> p s t"))
 
         def quantize_hidden(c):
-            tok = slice(c * OUT_TOK, (c + 1) * OUT_TOK)
-            nc.vector.quantize_mx(
-                out=h_codes[:, tok].bitcast(FP8X4),
-                scales=h_scale[:, tok],
-                in_=h_bf[:, tok, :].rearrange("p s t -> p (s t)"),
-            )
+            quantize(nc, h_words[:, tokens(c)], h_scales[:, tokens(c)], h_bf[c][:].rearrange("p s t -> p (s t)"))
 
-        def out_group(acc, m, tok):
+        def out_group(acc, m, c):
             cols = slice(m * P, (m + 1) * P)
-            nc.tensor.matmul_mx(
-                out=acc,
-                lhsT=w1_codes[:, cols].bitcast(FP8X4),
-                lhsT_scale=w1_scale[:, cols],
-                rhs=x_codes[:, tok].bitcast(FP8X4),
-                rhs_scale=x_scale[:, tok],
-                start=True,
-                stop=False,
-            )
-            nc.tensor.matmul_mx(
-                out=acc,
-                lhsT=w3_codes[:, cols].bitcast(FP8X4),
-                lhsT_scale=w3_scale[:, cols],
-                rhs=h_codes[:, tok].bitcast(FP8X4),
-                rhs_scale=h_scale[:, tok],
-                start=False,
-                stop=True,
-            )
+            mx_pass(nc, acc, w1_mx, cols, x_mx, tokens(c), True, False)
+            mx_pass(nc, acc, w3_mx, cols, h_mx, tokens(c), False, True)
 
-        def output(c, on_vector):
-            tok = slice(c * OUT_TOK, (c + 1) * OUT_TOK)
-            bank = psum.tile([P, N // P, OUT_TOK], F32, name="out_bank", tag="out_bank", bufs=3)
+        def output(c):
+            bank = psum.tile([P, N // P, CHUNKS[c]], F32, name="out_bank", tag="bank%d" % (starts[c] // BLOCK))
             for m in range(N // P):
-                out_group(bank[:, m, :], m, tok)
-            copy_on(nc, on_vector, result[c][:], bank[:])
-            nc.sync.dma_start(out=out_view[:, :, tok], in_=result[c][:])
+                out_group(bank[:, m, :], m, c)
+            copy_out_of_psum(nc, c == CHUNK_ON_VECTOR, result[c][:], bank[:])
+            nc.sync.dma_start(out=out_view[:, :, tokens(c)], in_=result[c][:])
 
-        def last_output(c):
-            tok = slice(c * OUT_TOK, (c + 1) * OUT_TOK)
+        def last_output():
+            c = len(CHUNKS) - 1
             for m in range(N // P):
-                bank = psum.tile([P, OUT_TOK], F32, name="last_bank", tag="h_bank", bufs=5)
-                out_group(bank[:], m, tok)
-                copy_on(nc, m == 1, result[c][:, m, :], bank[:])
-            nc.sync.dma_start(out=out_view[:, :, tok], in_=result[c][:])
+                bank = psum.tile([P, CHUNKS[c]], F32, name="last_bank", tag="bank%d" % (1 + 2 * m))
+                out_group(bank[:], m, c)
+                copy_out_of_psum(nc, m == 0, result[c][:, m, :], bank[:])
+            nc.sync.dma_start(out=out_view[:, :, tokens(c)], in_=result[c][:])
 
-        nc.scalar.copy(out=w3_dst, in_=w3_src)
         hidden(0)
-        hidden(1)
         nc.vector.tensor_copy(out=w1_dst, in_=w1_src)
-        quantize_weight(w3_bf, w3_codes, w3_scale)
-        quantize_weight(w1_bf, w1_codes, w1_scale)
         hidden(2)
+        hidden(1)
+        quantize(nc, w1_words[:], w1_scales[:], w1_bf[:].rearrange("p c j -> p (c j)"))
         hidden(3)
         quantize_hidden(0)
         hidden(4)
         hidden(5)
         quantize_hidden(1)
-        output(0, False)
         hidden(6)
-        hidden(7)
+        output(0)
         quantize_hidden(2)
-        output(1, False)
+        hidden(7)
         quantize_hidden(3)
-        output(2, True)
-        last_output(3)
+        quantize_hidden(4)
+        for c in range(1, len(CHUNKS) - 1):
+            output(c)
+        last_output()

@@ -24,9 +24,12 @@ BLOCK = 128
 LINE = 4
 
 CHUNKS = (256, 256, 256, 128, 128)
+STORE = 256
 
 BLOCKS_ON_VECTOR = (2, 5, 7)
-CHUNK_ON_VECTOR = 3
+CHUNKS_ON_VECTOR = (3, 4)
+
+W2_GROUPS_ON_VECTOR = 32
 
 W3_GROUPS_ON_VECTOR = 28
 
@@ -42,6 +45,7 @@ H1_AT = H2_AT + H_BYTES[2]
 H4_AT = H1_AT + H_BYTES[1]
 H_WORDS_AT = H4_AT + H_BYTES[4]
 W1_BF_AT = H_WORDS_AT + S * 4
+W3_BF_AT = W1_BF_AT + N * PACK * 2
 H_AT = (W3_RAW_AT, H1_AT, H2_AT, W1_BF_AT, H4_AT)
 
 
@@ -78,7 +82,7 @@ def tile_picked_lora_none_p_kernel(tc, x_words, x_scales, w1, w2, w3, offs, out)
         offsets = keep.tile([P, S // LIST_ROWS], U16, name="offsets")
         all_words = keep.tile([P, T], U32, name="all_words", align_bytes=ALIGN)
         all_scales = shared.tile([P, T], U8, name="all_scales", align_bytes=ALIGN, offset=SCALES_AT)
-        w2_raw = [keep.tile([P, PACK, H // 2], F32, name="w2_raw%d" % u, align_bytes=ALIGN) for u in range(2)]
+        w2_raw = keep.tile([P, PACK, H], F32, name="w2_raw", align_bytes=ALIGN)
         picked_words = keep.tile([P, S], U32, name="picked_words", align_bytes=ALIGN)
         picked_rows = keep.tile([P, S], U8, name="picked_rows", align_bytes=ALIGN)
         picked_scales = keep.tile([P, S], U8, name="picked_scales", align_bytes=ALIGN)
@@ -90,9 +94,7 @@ def tile_picked_lora_none_p_kernel(tc, x_words, x_scales, w1, w2, w3, offs, out)
             out=all_words[:].bitcast(I32),
             in_=x_words[0].rearrange("p c r -> p (c r)").bitcast(I32),
         )
-        w2_rows = w2.rearrange("(p j) c -> p j c", j=PACK)
-        for u in range(2):
-            nc.sync.dma_start(out=w2_raw[u][:], in_=w2_rows[:, :, u * (H // 2) : (u + 1) * (H // 2)])
+        nc.sync.dma_start(out=w2_raw[:], in_=w2.rearrange("(p j) c -> p j c", j=PACK))
         nc.vector.memset(all_scales[:first_row, :].bitcast(I32), 0)
         nc.vector.memset(picked_scales[:].bitcast(I32), 0)
 
@@ -126,16 +128,16 @@ def tile_picked_lora_none_p_kernel(tc, x_words, x_scales, w1, w2, w3, offs, out)
         w2_words = keep.tile([P, H], U32, name="w2_words", align_bytes=ALIGN)
         w2_scales = keep.tile([P, H], U8, name="w2_scales", align_bytes=ALIGN)
         w2_dst = w2_bf[:].rearrange("p t m j -> p m j t")
-        w2_src = [raw[:].rearrange("p j (m t) -> p m j t", t=PACK) for raw in w2_raw]
-        nc.scalar.copy(out=w2_dst[:, : P // 2], in_=w2_src[0])
-        nc.scalar.copy(out=w2_dst[:, P // 2 :, :, :2], in_=w2_src[1][:, :, :, :2])
-        nc.vector.tensor_copy(out=w2_dst[:, P // 2 :, :, 2:], in_=w2_src[1][:, :, :, 2:])
+        w2_src = w2_raw[:].rearrange("p j (m t) -> p m j t", t=PACK)
+        nc.scalar.copy(out=w2_dst[:, W2_GROUPS_ON_VECTOR:, :, 2:], in_=w2_src[:, W2_GROUPS_ON_VECTOR:, :, 2:])
+        nc.vector.tensor_copy(out=w2_dst[:, :, :, :2], in_=w2_src[:, :, :, :2])
+        nc.vector.tensor_copy(out=w2_dst[:, :W2_GROUPS_ON_VECTOR, :, 2:], in_=w2_src[:, :W2_GROUPS_ON_VECTOR, :, 2:])
         for t in (0, 2):
             cols = slice(t * P, (t + 2) * P)
             quantize(nc, w2_words[:, cols], w2_scales[:, cols], w2_bf[:, t : t + 2].rearrange("p t m j -> p (t m j)"))
         w2_mx = (w2_words, w2_scales)
 
-        w3_bf = keep.tile([P, N, PACK], BF16, name="w3_bf", align_bytes=ALIGN)
+        w3_bf = shared.tile([P, N, PACK], BF16, name="w3_bf", align_bytes=ALIGN, offset=W3_BF_AT)
         w3_words = keep.tile([P, N], U32, name="w3_words", align_bytes=ALIGN)
         w3_scales = keep.tile([P, N], U8, name="w3_scales", align_bytes=ALIGN)
         w1_bf = shared.tile([P, N, PACK], BF16, name="w1_bf", align_bytes=ALIGN, offset=W1_BF_AT)
@@ -157,7 +159,7 @@ def tile_picked_lora_none_p_kernel(tc, x_words, x_scales, w1, w2, w3, offs, out)
         h_words = shared.tile([P, S], U32, name="h_words", align_bytes=ALIGN, offset=H_WORDS_AT)
         h_scales = keep.tile([P, S], U8, name="h_scales", align_bytes=ALIGN)
         h_mx = (h_words, h_scales)
-        result = [keep.tile([P, N // P, n], F32, name="result%d" % c, align_bytes=ALIGN) for c, n in enumerate(CHUNKS)]
+        result = [keep.tile([P, N // P, STORE], F32, name="result%d" % r, align_bytes=ALIGN) for r in range(S // STORE)]
         out_view = out.rearrange("(m p) s -> p m s", p=P)
         starts = [sum(CHUNKS[:c]) for c in range(len(CHUNKS))]
 
@@ -185,23 +187,17 @@ def tile_picked_lora_none_p_kernel(tc, x_words, x_scales, w1, w2, w3, offs, out)
             bank = psum.tile([P, N // P, CHUNKS[c]], F32, name="out_bank", tag="bank%d" % (starts[c] // BLOCK))
             for m in range(N // P):
                 out_group(bank[:, m, :], m, c)
-            copy_out_of_psum(nc, c == CHUNK_ON_VECTOR, result[c][:], bank[:])
-            nc.sync.dma_start(out=out_view[:, :, tokens(c)], in_=result[c][:])
-
-        def last_output():
-            c = len(CHUNKS) - 1
-            for m in range(N // P):
-                bank = psum.tile([P, CHUNKS[c]], F32, name="last_bank", tag="bank%d" % (1 + 2 * m))
-                out_group(bank[:], m, c)
-                copy_out_of_psum(nc, m == 0, result[c][:, m, :], bank[:])
-            nc.sync.dma_start(out=out_view[:, :, tokens(c)], in_=result[c][:])
+            r, first = divmod(starts[c], STORE)
+            copy_out_of_psum(nc, c in CHUNKS_ON_VECTOR, result[r][:, :, first : first + CHUNKS[c]], bank[:])
+            if first + CHUNKS[c] == STORE:
+                nc.sync.dma_start(out=out_view[:, :, r * STORE : (r + 1) * STORE], in_=result[r][:])
 
         hidden(0)
+        hidden(1)
         nc.vector.tensor_copy(out=w1_dst, in_=w1_src)
         hidden(2)
-        hidden(1)
-        quantize(nc, w1_words[:], w1_scales[:], w1_bf[:].rearrange("p c j -> p (c j)"))
         hidden(3)
+        quantize(nc, w1_words[:], w1_scales[:], w1_bf[:].rearrange("p c j -> p (c j)"))
         quantize_hidden(0)
         hidden(4)
         hidden(5)
@@ -212,6 +208,5 @@ def tile_picked_lora_none_p_kernel(tc, x_words, x_scales, w1, w2, w3, offs, out)
         hidden(7)
         quantize_hidden(3)
         quantize_hidden(4)
-        for c in range(1, len(CHUNKS) - 1):
+        for c in range(1, len(CHUNKS)):
             output(c)
-        last_output()

from contextlib import ExitStack

import concourse.mybir as mybir

K, T, S, H, N = 512, 4096, 1024, 512, 256
FLOPS = 2 * S * (K * H + K * N + H * N)

F32 = mybir.dt.float32
BF16 = mybir.dt.bfloat16
I32 = mybir.dt.int32
U32 = mybir.dt.uint32
U16 = mybir.dt.uint16
U8 = mybir.dt.uint8
FP8X4 = mybir.dt.float8_e4m3fn_x4

P = 128
PACK = 4
ALIGN = 64
SCALE_ROWS = K // 32
QUADRANT = 32
LIST_ROWS = 16
GATHER = 512
BLOCK = 128
LINE = 4

CHUNKS = (256, 256, 256, 128, 128)
STORE = 256

BLOCKS_ON_VECTOR = (2, 5, 7)
CHUNKS_ON_VECTOR = (3, 4)

W2_GROUPS_ON_VECTOR = 32

W3_GROUPS_ON_VECTOR = 28

WARM_UP_PASSES = 3

RAW_BYTES = PACK * N * 4
H_BYTES = [n * PACK * 2 for n in CHUNKS]
W3_RAW_AT = 0
W1_RAW_AT = RAW_BYTES
SCALES_AT = RAW_BYTES // 2
H2_AT = W1_RAW_AT + ALIGN - H_BYTES[2]
H1_AT = H2_AT + H_BYTES[2]
H4_AT = H1_AT + H_BYTES[1]
H_WORDS_AT = H4_AT + H_BYTES[4]
W1_BF_AT = H_WORDS_AT + S * 4
W3_BF_AT = W1_BF_AT + N * PACK * 2
H_AT = (W3_RAW_AT, H1_AT, H2_AT, W1_BF_AT, H4_AT)


def copy_out_of_psum(nc, on_vector, out, in_):
    if on_vector:
        nc.vector.tensor_copy(out=out, in_=in_)
    else:
        nc.scalar.copy(out=out, in_=in_)


def quantize(nc, words, scales, values):
    nc.vector.quantize_mx(out=words.bitcast(FP8X4), scales=scales, in_=values)


def mx_pass(nc, acc, stationary, stationary_cols, moving, moving_cols, start, stop):
    nc.tensor.matmul_mx(
        out=acc,
        lhsT=stationary[0][:, stationary_cols].bitcast(FP8X4),
        lhsT_scale=stationary[1][:, stationary_cols],
        rhs=moving[0][:, moving_cols].bitcast(FP8X4),
        rhs_scale=moving[1][:, moving_cols],
        start=start,
        stop=stop,
    )


def tile_picked_lora_none_p_kernel(tc, x_words, x_scales, w1, w2, w3, offs, out):
    nc = tc.nc
    with ExitStack() as ctx:
        keep = ctx.enter_context(tc.tile_pool(name="keep", bufs=1))
        shared = ctx.enter_context(tc.tile_pool(name="shared", bufs=1))
        psum = ctx.enter_context(tc.psum_pool(name="psum", bufs=1))

        offsets = keep.tile([P, S // LIST_ROWS], U16, name="offsets")
        all_words = keep.tile([P, T], U32, name="all_words", align_bytes=ALIGN)
        all_scales = shared.tile([P, T], U8, name="all_scales", align_bytes=ALIGN, offset=SCALES_AT)
        w2_raw = keep.tile([P, PACK, H], F32, name="w2_raw", align_bytes=ALIGN)
        picked_words = keep.tile([P, S], U32, name="picked_words", align_bytes=ALIGN)
        picked_rows = keep.tile([P, S], U8, name="picked_rows", align_bytes=ALIGN)
        picked_scales = keep.tile([P, S], U8, name="picked_scales", align_bytes=ALIGN)

        first_row = P - SCALE_ROWS
        nc.sync.dma_start(out=all_scales[first_row:, :].bitcast(I32), in_=x_scales[0].bitcast(I32))
        nc.sync.dma_start(offsets[:], offs)
        nc.sync.dma_start(
            out=all_words[:].bitcast(I32),
            in_=x_words[0].rearrange("p c r -> p (c r)").bitcast(I32),
        )
        nc.sync.dma_start(out=w2_raw[:], in_=w2.rearrange("(p j) c -> p j c", j=PACK))
        nc.vector.memset(all_scales[:first_row, :].bitcast(I32), 0)
        nc.vector.memset(picked_scales[:].bitcast(I32), 0)

        nc.vector.tensor_copy(picked_rows[:], all_scales[:].indirect(offsets[:]))
        rows = SCALE_ROWS * QUADRANT // P
        for q in range(P // QUADRANT):
            nc.sync.dma_start(
                out=picked_scales[QUADRANT * q : QUADRANT * q + rows, :].bitcast(I32),
                in_=picked_rows[first_row + rows * q : first_row + rows * (q + 1), :].bitcast(I32),
            )
        w3_raw = shared.tile([P, PACK * N], F32, name="w3_raw", align_bytes=ALIGN, offset=W3_RAW_AT)
        w1_raw = shared.tile([P, PACK * N], F32, name="w1_raw", align_bytes=ALIGN, offset=W1_RAW_AT)
        for raw, w in ((w3_raw, w3), (w1_raw, w1)):
            nc.sync.dma_start(out=raw[:], in_=w.rearrange("(p j) c -> p (j c)", j=PACK))

        list_cols = GATHER // LIST_ROWS
        for g in range(S // GATHER):
            nc.vector.tensor_copy(
                picked_words[:, g * GATHER : (g + 1) * GATHER],
                all_words[:].indirect(offsets[:, g * list_cols : (g + 1) * list_cols]),
            )
        x_mx = (picked_words, picked_scales)

        blocks = S // BLOCK
        warm_up = psum.tile([P, GATHER], F32, name="warm_up", tag="bank%d" % (blocks - 1))
        first_words = (picked_words, picked_rows)
        for i in range(WARM_UP_PASSES):
            mx_pass(nc, warm_up[:], first_words, slice(0, P), first_words, slice(0, GATHER), True, True)

        w2_bf = keep.tile([P, PACK, P, PACK], BF16, name="w2_bf", align_bytes=ALIGN)
        w2_words = keep.tile([P, H], U32, name="w2_words", align_bytes=ALIGN)
        w2_scales = keep.tile([P, H], U8, name="w2_scales", align_bytes=ALIGN)
        w2_dst = w2_bf[:].rearrange("p t m j -> p m j t")
        w2_src = w2_raw[:].rearrange("p j (m t) -> p m j t", t=PACK)
        nc.scalar.copy(out=w2_dst[:, W2_GROUPS_ON_VECTOR:, :, 2:], in_=w2_src[:, W2_GROUPS_ON_VECTOR:, :, 2:])
        nc.vector.tensor_copy(out=w2_dst[:, :, :, :2], in_=w2_src[:, :, :, :2])
        nc.vector.tensor_copy(out=w2_dst[:, :W2_GROUPS_ON_VECTOR, :, 2:], in_=w2_src[:, :W2_GROUPS_ON_VECTOR, :, 2:])
        for t in (0, 2):
            cols = slice(t * P, (t + 2) * P)
            quantize(nc, w2_words[:, cols], w2_scales[:, cols], w2_bf[:, t : t + 2].rearrange("p t m j -> p (t m j)"))
        w2_mx = (w2_words, w2_scales)

        w3_bf = shared.tile([P, N, PACK], BF16, name="w3_bf", align_bytes=ALIGN, offset=W3_BF_AT)
        w3_words = keep.tile([P, N], U32, name="w3_words", align_bytes=ALIGN)
        w3_scales = keep.tile([P, N], U8, name="w3_scales", align_bytes=ALIGN)
        w1_bf = shared.tile([P, N, PACK], BF16, name="w1_bf", align_bytes=ALIGN, offset=W1_BF_AT)
        w1_words = keep.tile([P, N], U32, name="w1_words", align_bytes=ALIGN)
        w1_scales = keep.tile([P, N], U8, name="w1_scales", align_bytes=ALIGN)
        w3_dst, w1_dst = [bf[:].rearrange("p (c i) j -> p c j i", i=LINE) for bf in (w3_bf, w1_bf)]
        w3_src, w1_src = [raw[:].rearrange("p (j c i) -> p c j i", j=PACK, i=LINE) for raw in (w3_raw, w1_raw)]
        w3_mx = (w3_words, w3_scales)
        w1_mx = (w1_words, w1_scales)

        nc.scalar.copy(out=w3_dst[:, W3_GROUPS_ON_VECTOR:], in_=w3_src[:, W3_GROUPS_ON_VECTOR:])
        nc.vector.tensor_copy(out=w3_dst[:, :W3_GROUPS_ON_VECTOR], in_=w3_src[:, :W3_GROUPS_ON_VECTOR])
        quantize(nc, w3_words[:], w3_scales[:], w3_bf[:].rearrange("p c j -> p (c j)"))

        h_bf = [
            shared.tile([P, n, PACK], BF16, name="h_bf%d" % c, align_bytes=ALIGN, offset=H_AT[c])
            for c, n in enumerate(CHUNKS)
        ]
        h_words = shared.tile([P, S], U32, name="h_words", align_bytes=ALIGN, offset=H_WORDS_AT)
        h_scales = keep.tile([P, S], U8, name="h_scales", align_bytes=ALIGN)
        h_mx = (h_words, h_scales)
        result = [keep.tile([P, N // P, STORE], F32, name="result%d" % r, align_bytes=ALIGN) for r in range(S // STORE)]
        out_view = out.rearrange("(m p) s -> p m s", p=P)
        starts = [sum(CHUNKS[:c]) for c in range(len(CHUNKS))]

        def tokens(c):
            return slice(starts[c], starts[c] + CHUNKS[c])

        def hidden(b):
            first = b * BLOCK
            bank = psum.tile([P, PACK, BLOCK], F32, name="h_bank", tag="bank%d" % b)
            for t in range(PACK):
                mx_pass(nc, bank[:, t, :], w2_mx, slice(t * P, (t + 1) * P), x_mx, slice(first, first + BLOCK), True, True)
            c = max(i for i, start in enumerate(starts) if start <= first)
            dst = h_bf[c][:, first - starts[c] : first - starts[c] + BLOCK, :]
            copy_out_of_psum(nc, b in BLOCKS_ON_VECTOR, dst, bank[:].rearrange("p t s -> p s t"))

        def quantize_hidden(c):
            quantize(nc, h_words[:, tokens(c)], h_scales[:, tokens(c)], h_bf[c][:].rearrange("p s t -> p (s t)"))

        def out_group(acc, m, c):
            cols = slice(m * P, (m + 1) * P)
            mx_pass(nc, acc, w1_mx, cols, x_mx, tokens(c), True, False)
            mx_pass(nc, acc, w3_mx, cols, h_mx, tokens(c), False, True)

        def output(c):
            bank = psum.tile([P, N // P, CHUNKS[c]], F32, name="out_bank", tag="bank%d" % (starts[c] // BLOCK))
            for m in range(N // P):
                out_group(bank[:, m, :], m, c)
            r, first = divmod(starts[c], STORE)
            copy_out_of_psum(nc, c in CHUNKS_ON_VECTOR, result[r][:, :, first : first + CHUNKS[c]], bank[:])
            if first + CHUNKS[c] == STORE:
                nc.sync.dma_start(out=out_view[:, :, r * STORE : (r + 1) * STORE], in_=result[r][:])

        hidden(0)
        hidden(1)
        nc.vector.tensor_copy(out=w1_dst, in_=w1_src)
        hidden(2)
        hidden(3)
        quantize(nc, w1_words[:], w1_scales[:], w1_bf[:].rearrange("p c j -> p (c j)"))
        quantize_hidden(0)
        hidden(4)
        hidden(5)
        quantize_hidden(1)
        hidden(6)
        output(0)
        quantize_hidden(2)
        hidden(7)
        quantize_hidden(3)
        quantize_hidden(4)
        for c in range(1, len(CHUNKS)):
            output(c)
